import numpy as np
import ml_dtypes


def mxq(x, axis, fmt="e4m3"):
    dtype, down = {"e4m3": (ml_dtypes.float8_e4m3fn, 7), "e5m2": (ml_dtypes.float8_e5m2, 14)}[fmt]
    v = np.moveaxis(np.asarray(x, np.float32).astype(ml_dtypes.bfloat16).astype(np.float64), axis, -1)
    blocks = v.reshape(v.shape[:-1] + (-1, 32))
    amax = np.abs(blocks).max(-1, keepdims=True)
    byte = np.maximum(np.where(amax > 0, np.frexp(amax)[1] - 1 + 127, 0) - down, 1)
    scale = np.exp2(byte - 127.0)
    codes = (blocks / scale).astype(np.float32).astype(dtype).astype(np.float64)
    return np.moveaxis((codes * scale).reshape(v.shape), -1, axis)


WIDE = False


def mx_kscale(k, group=512):
    if not WIDE:
        return np.ones(k)
    levels = np.array([18, -18])
    if group != 512:
        return np.exp2(np.random.permutation(np.resize(levels, k // group))).repeat(group)
    if k % 512:
        return np.exp2(np.random.permutation(np.resize(levels, k // 32))).repeat(32)
    a = np.empty((k // 512, 16))
    for p in range(k // 512):
        a[p, :8] = np.random.permutation(np.resize(levels, 8))
        for g in range(8):
            far = levels[np.abs(levels - a[p, g]) >= 10]
            a[p, g + 8] = far[np.random.randint(len(far))]
    return np.exp2(a.ravel()).repeat(32)


def f64(x):
    return np.asarray(x).astype(np.float64)


def silu(v):
    return v / (1.0 + np.exp(-v))


G, D, M, N = 8, 128, 128, 512


def setup_inputs():
    n = np.random.standard_normal
    s = mx_kscale(D, 0)[:, None]
    return {
        "x": (n((G, D, N)) * s).astype(np.float32),
        "w": (n((G, D, M)) / np.sqrt(D) / s).astype(np.float32),
        "r": n((G, M, N)).astype(np.float32),
    }


def reference(x, w, r):
    xq = mxq(f64(x), 1, "e4m3")
    y = mxq(f64(w), 1, "e4m3").transpose(0, 2, 1) @ xq
    y = silu(y)
    y = y + f64(r)
    return y

@@ -1,0 +1,95 @@
+from contextlib import ExitStack
+
+import concourse.mybir as mybir
+
+G, D, M, N = 8, 128, 128, 512
+FLOPS = 2 * G * D * M * N
+
+F32 = mybir.dt.float32
+BF16 = mybir.dt.bfloat16
+U32 = mybir.dt.uint32
+U8 = mybir.dt.uint8
+FP8X4 = mybir.dt.float8_e4m3fn_x4
+SILU = mybir.ActivationFunctionType.Silu
+ADD = mybir.AluOpType.add
+
+P = 128
+PACK = 4
+ROWS = D // PACK
+SIDE = P // ROWS
+SETS = G // SIDE
+RUN = 4
+PAIR = 2
+
+
+def tile_rows_glin_silu_res_kernel(tc, x, w, r, out):
+    nc = tc.nc
+    x_sets = x.rearrange("g d n -> (g d) n").rearrange("(s p j) n -> s p j n", p=P, j=PACK)
+    w_all = w.rearrange("g d m -> (g d) m").rearrange("(s p j) m -> p s (j m)", p=P, j=PACK)
+
+    with ExitStack() as ctx:
+        sb = ctx.enter_context(tc.tile_pool(name="sb", bufs=1))
+        ps = ctx.enter_context(tc.psum_pool(name="ps", bufs=1))
+        ctx.enter_context(tc.manual_schedule())
+
+        x_raw = [sb.tile([P, PACK, N], F32, name="x_raw%d" % s) for s in range(SETS)]
+        w_raw = sb.tile([P, SETS, PACK * M], F32, name="w_raw")
+        res = [sb.tile([P, PAIR, N], F32, name="res%d" % h) for h in range(G // PAIR)]
+        x_bf = [sb.tile([P, N * PACK], BF16, name="x_bf%d" % s, align_bytes=64) for s in range(SETS)]
+        w_bf = sb.tile([P, SETS * M * PACK], BF16, name="w_bf", align_bytes=64)
+        x_codes = [sb.tile([P, N], U32, name="x_codes%d" % s, align_bytes=64) for s in range(SETS)]
+        x_scales = [sb.tile([P, N], U8, name="x_scales%d" % s, align_bytes=64) for s in range(SETS)]
+        w_codes = sb.tile([P, SETS * M], U32, name="w_codes", align_bytes=64)
+        w_scales = sb.tile([P, SETS * M], U8, name="w_scales", align_bytes=64)
+        acc = [ps.tile([M, N], F32, name="acc%d" % g) for g in range(G)]
+        act = [sb.tile([M, N], F32, name="act%d" % g) for g in range(G)]
+
+        nc.sync.dma_start(out=x_raw[0][:], in_=x_sets[0])
+        nc.sync.dma_start(out=w_raw[:], in_=w_all)
+        nc.sync.dma_start(out=x_raw[1][:], in_=x_sets[1])
+        for h in range(G // PAIR):
+            nc.sync.dma_start(out=res[h][:], in_=r[PAIR * h : PAIR * (h + 1)].rearrange("g m n -> m g n"))
+
+        def interleave_x(s):
+            nc.vector.tensor_copy(
+                out=x_bf[s][:].rearrange("p (a i j) -> p a j i", i=RUN, j=PACK),
+                in_=x_raw[s][:].rearrange("p j (a i) -> p a j i", i=RUN),
+            )
+
+        def interleave_w():
+            nc.vector.tensor_copy(
+                out=w_bf[:].rearrange("p (s a i j) -> p s a j i", s=SETS, i=RUN, j=PACK),
+                in_=w_raw[:].rearrange("p s (j a i) -> p s a j i", i=RUN, j=PACK),
+            )
+
+        def quantize(codes, scales, values):
+            nc.vector.quantize_mx(out=codes[:].bitcast(FP8X4), scales=scales[:], in_=values[:])
+
+        def products(s):
+            cols = slice(s * M, (s + 1) * M)
+            for c in range(SIDE):
+                rows = slice(ROWS * c, ROWS * (c + 1))
+                nc.tensor.matmul_mx(
+                    out=acc[SIDE * s + c][:],
+                    lhsT=w_codes[rows, cols].bitcast(FP8X4),
+                    lhsT_scale=w_scales[rows, cols],
+                    rhs=x_codes[s][rows, :].bitcast(FP8X4),
+                    rhs_scale=x_scales[s][rows, :],
+                    start=True,
+                    stop=True,
+                )
+            for c in range(SIDE):
+                g = SIDE * s + c
+                nc.scalar.activation(out=act[g][:], in_=acc[g][:], func=SILU)
+
+        interleave_x(0)
+        interleave_w()
+        quantize(x_codes[0], x_scales[0], x_bf[0])
+        quantize(w_codes, w_scales, w_bf)
+        products(0)
+        interleave_x(1)
+        quantize(x_codes[1], x_scales[1], x_bf[1])
+        products(1)
+        for g in range(G):
+            nc.vector.tensor_tensor(out=act[g][:], in0=act[g][:], in1=res[g // PAIR][:, g % PAIR, :], op=ADD)
+            nc.sync.dma_start(out=out[g], in_=act[g][:])

@@ -20,6 +20,9 @@ SIDE = P // ROWS
 SETS = G // SIDE
 RUN = 4
 PAIR = 2
+HALF = N // 2
+SPLIT = 320
+RES_CHUNKS = ((0, 2), (2, 5), (5, 8))
 
 
 def tile_rows_glin_silu_res_kernel(tc, x, w, r, out):
@@ -34,7 +37,8 @@ def tile_rows_glin_silu_res_kernel(tc, x, w, r, out):
 
         x_raw = [sb.tile([P, PACK, N], F32, name="x_raw%d" % s) for s in range(SETS)]
         w_raw = sb.tile([P, SETS, PACK * M], F32, name="w_raw")
-        res = [sb.tile([P, PAIR, N], F32, name="res%d" % h) for h in range(G // PAIR)]
+        res = [sb.tile([M, b - a, N], F32, name="res%d" % a) for a, b in RES_CHUNKS]
+        res_of = [res[h][:, g - a, :] for h, (a, b) in enumerate(RES_CHUNKS) for g in range(a, b)]
         x_bf = [sb.tile([P, N * PACK], BF16, name="x_bf%d" % s, align_bytes=64) for s in range(SETS)]
         w_bf = sb.tile([P, SETS * M * PACK], BF16, name="w_bf", align_bytes=64)
         x_codes = [sb.tile([P, N], U32, name="x_codes%d" % s, align_bytes=64) for s in range(SETS)]
@@ -42,18 +46,22 @@ def tile_rows_glin_silu_res_kernel(tc, x, w, r, out):
         w_codes = sb.tile([P, SETS * M], U32, name="w_codes", align_bytes=64)
         w_scales = sb.tile([P, SETS * M], U8, name="w_scales", align_bytes=64)
         acc = [ps.tile([M, N], F32, name="acc%d" % g) for g in range(G)]
-        act = [sb.tile([M, N], F32, name="act%d" % g) for g in range(G)]
+        act = [sb.tile([M, PAIR, N], F32, name="act%d" % h) for h in range(G // PAIR)]
+
+        warm = sb.tile([P, 8], F32, name="warm")
+        nc.vector.memset(warm[:], 0.0)
+        nc.scalar.activation(out=warm[:], in_=warm[:], func=SILU)
 
         nc.sync.dma_start(out=x_raw[0][:], in_=x_sets[0])
         nc.sync.dma_start(out=w_raw[:], in_=w_all)
         nc.sync.dma_start(out=x_raw[1][:], in_=x_sets[1])
-        for h in range(G // PAIR):
-            nc.sync.dma_start(out=res[h][:], in_=r[PAIR * h : PAIR * (h + 1)].rearrange("g m n -> m g n"))
+        for h, (a, b) in enumerate(RES_CHUNKS):
+            nc.sync.dma_start(out=res[h][:], in_=r[a:b].rearrange("g m n -> m g n"))
 
-        def interleave_x(s):
-            nc.vector.tensor_copy(
-                out=x_bf[s][:].rearrange("p (a i j) -> p a j i", i=RUN, j=PACK),
-                in_=x_raw[s][:].rearrange("p j (a i) -> p a j i", i=RUN),
+        def interleave_x(copy, s, a, b):
+            copy(
+                out=x_bf[s][:, PACK * a : PACK * b].rearrange("p (a i j) -> p a j i", i=RUN, j=PACK),
+                in_=x_raw[s][:, :, a:b].rearrange("p j (a i) -> p a j i", i=RUN),
             )
 
         def interleave_w():
@@ -62,8 +70,12 @@ def tile_rows_glin_silu_res_kernel(tc, x, w, r, out):
                 in_=w_raw[:].rearrange("p s (j a i) -> p s a j i", i=RUN, j=PACK),
             )
 
-        def quantize(codes, scales, values):
-            nc.vector.quantize_mx(out=codes[:].bitcast(FP8X4), scales=scales[:], in_=values[:])
+        def quantize_x(s, a, b):
+            nc.vector.quantize_mx(
+                out=x_codes[s][:, a:b].bitcast(FP8X4),
+                scales=x_scales[s][:, a:b],
+                in_=x_bf[s][:, PACK * a : PACK * b],
+            )
 
         def products(s):
             cols = slice(s * M, (s + 1) * M)
@@ -78,18 +90,21 @@ def tile_rows_glin_silu_res_kernel(tc, x, w, r, out):
                     start=True,
                     stop=True,
                 )
-            for c in range(SIDE):
-                g = SIDE * s + c
-                nc.scalar.activation(out=act[g][:], in_=acc[g][:], func=SILU)
 
-        interleave_x(0)
+        interleave_x(nc.vector.tensor_copy, 0, 0, N)
         interleave_w()
-        quantize(x_codes[0], x_scales[0], x_bf[0])
-        quantize(w_codes, w_scales, w_bf)
+        quantize_x(0, 0, N)
+        nc.vector.quantize_mx(out=w_codes[:].bitcast(FP8X4), scales=w_scales[:], in_=w_bf[:])
         products(0)
-        interleave_x(1)
-        quantize(x_codes[1], x_scales[1], x_bf[1])
+        interleave_x(nc.scalar.copy, 1, SPLIT, N)
+        interleave_x(nc.vector.tensor_copy, 1, 0, HALF)
+        interleave_x(nc.vector.tensor_copy, 1, HALF, SPLIT)
+        quantize_x(1, 0, HALF)
+        quantize_x(1, HALF, N)
         products(1)
         for g in range(G):
-            nc.vector.tensor_tensor(out=act[g][:], in0=act[g][:], in1=res[g // PAIR][:, g % PAIR, :], op=ADD)
-            nc.sync.dma_start(out=out[g], in_=act[g][:])
+            nc.scalar.activation(out=act[g // PAIR][:, g % PAIR, :], in_=acc[g][:], func=SILU)
+        for h in range(G // PAIR):
+            for i in range(PAIR):
+                nc.vector.tensor_tensor(out=act[h][:, i, :], in0=act[h][:, i, :], in1=res_of[PAIR * h + i], op=ADD)
+            nc.sync.dma_start(out=out[PAIR * h : PAIR * (h + 1)].rearrange("g m n -> m g n"), in_=act[h][:])

@@ -19,10 +19,9 @@ ROWS = D // PACK
 SIDE = P // ROWS
 SETS = G // SIDE
 RUN = 4
-PAIR = 2
 HALF = N // 2
 SPLIT = 320
-RES_CHUNKS = ((0, 2), (2, 5), (5, 8))
+RES_CHUNKS = ((0, 1), (1, 3), (3, 5), (5, 7), (7, 8))
 
 
 def tile_rows_glin_silu_res_kernel(tc, x, w, r, out):
@@ -40,13 +39,13 @@ def tile_rows_glin_silu_res_kernel(tc, x, w, r, out):
         res = [sb.tile([M, b - a, N], F32, name="res%d" % a) for a, b in RES_CHUNKS]
         res_of = [res[h][:, g - a, :] for h, (a, b) in enumerate(RES_CHUNKS) for g in range(a, b)]
         x_bf = [sb.tile([P, N * PACK], BF16, name="x_bf%d" % s, align_bytes=64) for s in range(SETS)]
-        w_bf = sb.tile([P, SETS * M * PACK], BF16, name="w_bf", align_bytes=64)
+        w_bf = [sb.tile([P, M * PACK], BF16, name="w_bf%d" % s, align_bytes=64) for s in range(SETS)]
         x_codes = [sb.tile([P, N], U32, name="x_codes%d" % s, align_bytes=64) for s in range(SETS)]
         x_scales = [sb.tile([P, N], U8, name="x_scales%d" % s, align_bytes=64) for s in range(SETS)]
-        w_codes = sb.tile([P, SETS * M], U32, name="w_codes", align_bytes=64)
-        w_scales = sb.tile([P, SETS * M], U8, name="w_scales", align_bytes=64)
+        w_codes = [sb.tile([P, M], U32, name="w_codes%d" % s, align_bytes=64) for s in range(SETS)]
+        w_scales = [sb.tile([P, M], U8, name="w_scales%d" % s, align_bytes=64) for s in range(SETS)]
         acc = [ps.tile([M, N], F32, name="acc%d" % g) for g in range(G)]
-        act = [sb.tile([M, PAIR, N], F32, name="act%d" % h) for h in range(G // PAIR)]
+        act = [sb.tile([M, N], F32, name="act%d" % g) for g in range(G)]
 
         warm = sb.tile([P, 8], F32, name="warm")
         nc.vector.memset(warm[:], 0.0)
@@ -64,11 +63,14 @@ def tile_rows_glin_silu_res_kernel(tc, x, w, r, out):
                 in_=x_raw[s][:, :, a:b].rearrange("p j (a i) -> p a j i", i=RUN),
             )
 
-        def interleave_w():
-            nc.vector.tensor_copy(
-                out=w_bf[:].rearrange("p (s a i j) -> p s a j i", s=SETS, i=RUN, j=PACK),
-                in_=w_raw[:].rearrange("p s (j a i) -> p s a j i", i=RUN, j=PACK),
+        def interleave_w(copy, s):
+            copy(
+                out=w_bf[s][:].rearrange("p (a i j) -> p a j i", i=RUN, j=PACK),
+                in_=w_raw[:, s, :].rearrange("p (j a i) -> p a j i", i=RUN, j=PACK),
             )
+
+        def quantize_w(s):
+            nc.vector.quantize_mx(out=w_codes[s][:].bitcast(FP8X4), scales=w_scales[s][:], in_=w_bf[s][:])
 
         def quantize_x(s, a, b):
             nc.vector.quantize_mx(
@@ -78,33 +80,42 @@ def tile_rows_glin_silu_res_kernel(tc, x, w, r, out):
             )
 
         def products(s):
-            cols = slice(s * M, (s + 1) * M)
             for c in range(SIDE):
                 rows = slice(ROWS * c, ROWS * (c + 1))
                 nc.tensor.matmul_mx(
                     out=acc[SIDE * s + c][:],
-                    lhsT=w_codes[rows, cols].bitcast(FP8X4),
-                    lhsT_scale=w_scales[rows, cols],
+                    lhsT=w_codes[s][rows, :].bitcast(FP8X4),
+                    lhsT_scale=w_scales[s][rows, :],
                     rhs=x_codes[s][rows, :].bitcast(FP8X4),
                     rhs_scale=x_scales[s][rows, :],
                     start=True,
                     stop=True,
                 )
 
-        interleave_x(nc.vector.tensor_copy, 0, 0, N)
-        interleave_w()
-        quantize_x(0, 0, N)
-        nc.vector.quantize_mx(out=w_codes[:].bitcast(FP8X4), scales=w_scales[:], in_=w_bf[:])
+        def silu(g):
+            nc.scalar.activation(out=act[g][:], in_=acc[g][:], func=SILU)
+
+        def finish(g):
+            nc.vector.tensor_tensor(out=act[g][:], in0=act[g][:], in1=res_of[g], op=ADD)
+            nc.sync.dma_start(out=out[g], in_=act[g][:])
+
+        interleave_x(nc.scalar.copy, 0, SPLIT, N)
+        interleave_x(nc.vector.tensor_copy, 0, 0, HALF)
+        interleave_x(nc.vector.tensor_copy, 0, HALF, SPLIT)
+        quantize_x(0, 0, HALF)
+        quantize_x(0, HALF, N)
+        interleave_w(nc.scalar.copy, 0)
+        quantize_w(0)
         products(0)
-        interleave_x(nc.scalar.copy, 1, SPLIT, N)
+        interleave_w(nc.vector.tensor_copy, 1)
+        quantize_w(1)
+        silu(0)
+        interleave_x(nc.scalar.copy, 1, HALF, N)
         interleave_x(nc.vector.tensor_copy, 1, 0, HALF)
-        interleave_x(nc.vector.tensor_copy, 1, HALF, SPLIT)
+        finish(0)
         quantize_x(1, 0, HALF)
         quantize_x(1, HALF, N)
         products(1)
-        for g in range(G):
-            nc.scalar.activation(out=act[g // PAIR][:, g % PAIR, :], in_=acc[g][:], func=SILU)
-        for h in range(G // PAIR):
-            for i in range(PAIR):
-                nc.vector.tensor_tensor(out=act[h][:, i, :], in0=act[h][:, i, :], in1=res_of[PAIR * h + i], op=ADD)
-            nc.sync.dma_start(out=out[PAIR * h : PAIR * (h + 1)].rearrange("g m n -> m g n"), in_=act[h][:])
+        for g in range(1, G):
+            silu(g)
+            finish(g)

from contextlib import ExitStack

import concourse.mybir as mybir

G, D, M, N = 8, 128, 128, 512
FLOPS = 2 * G * D * M * N

F32 = mybir.dt.float32
BF16 = mybir.dt.bfloat16
U32 = mybir.dt.uint32
U8 = mybir.dt.uint8
FP8X4 = mybir.dt.float8_e4m3fn_x4
SILU = mybir.ActivationFunctionType.Silu
ADD = mybir.AluOpType.add

P = 128
PACK = 4
ROWS = D // PACK
SIDE = P // ROWS
SETS = G // SIDE
RUN = 4
HALF = N // 2
SPLIT = 320
RES_CHUNKS = ((0, 1), (1, 3), (3, 5), (5, 7), (7, 8))


def tile_rows_glin_silu_res_kernel(tc, x, w, r, out):
    nc = tc.nc
    x_sets = x.rearrange("g d n -> (g d) n").rearrange("(s p j) n -> s p j n", p=P, j=PACK)
    w_all = w.rearrange("g d m -> (g d) m").rearrange("(s p j) m -> p s (j m)", p=P, j=PACK)

    with ExitStack() as ctx:
        sb = ctx.enter_context(tc.tile_pool(name="sb", bufs=1))
        ps = ctx.enter_context(tc.psum_pool(name="ps", bufs=1))
        ctx.enter_context(tc.manual_schedule())

        x_raw = [sb.tile([P, PACK, N], F32, name="x_raw%d" % s) for s in range(SETS)]
        w_raw = sb.tile([P, SETS, PACK * M], F32, name="w_raw")
        res = [sb.tile([M, b - a, N], F32, name="res%d" % a) for a, b in RES_CHUNKS]
        res_of = [res[h][:, g - a, :] for h, (a, b) in enumerate(RES_CHUNKS) for g in range(a, b)]
        x_bf = [sb.tile([P, N * PACK], BF16, name="x_bf%d" % s, align_bytes=64) for s in range(SETS)]
        w_bf = [sb.tile([P, M * PACK], BF16, name="w_bf%d" % s, align_bytes=64) for s in range(SETS)]
        x_codes = [sb.tile([P, N], U32, name="x_codes%d" % s, align_bytes=64) for s in range(SETS)]
        x_scales = [sb.tile([P, N], U8, name="x_scales%d" % s, align_bytes=64) for s in range(SETS)]
        w_codes = [sb.tile([P, M], U32, name="w_codes%d" % s, align_bytes=64) for s in range(SETS)]
        w_scales = [sb.tile([P, M], U8, name="w_scales%d" % s, align_bytes=64) for s in range(SETS)]
        acc = [ps.tile([M, N], F32, name="acc%d" % g) for g in range(G)]
        act = [sb.tile([M, N], F32, name="act%d" % g) for g in range(G)]

        warm = sb.tile([P, 8], F32, name="warm")
        nc.vector.memset(warm[:], 0.0)
        nc.scalar.activation(out=warm[:], in_=warm[:], func=SILU)

        nc.sync.dma_start(out=x_raw[0][:], in_=x_sets[0])
        nc.sync.dma_start(out=w_raw[:], in_=w_all)
        nc.sync.dma_start(out=x_raw[1][:], in_=x_sets[1])
        for h, (a, b) in enumerate(RES_CHUNKS):
            nc.sync.dma_start(out=res[h][:], in_=r[a:b].rearrange("g m n -> m g n"))

        def interleave_x(copy, s, a, b):
            copy(
                out=x_bf[s][:, PACK * a : PACK * b].rearrange("p (a i j) -> p a j i", i=RUN, j=PACK),
                in_=x_raw[s][:, :, a:b].rearrange("p j (a i) -> p a j i", i=RUN),
            )

        def interleave_w(copy, s):
            copy(
                out=w_bf[s][:].rearrange("p (a i j) -> p a j i", i=RUN, j=PACK),
                in_=w_raw[:, s, :].rearrange("p (j a i) -> p a j i", i=RUN, j=PACK),
            )

        def quantize_w(s):
            nc.vector.quantize_mx(out=w_codes[s][:].bitcast(FP8X4), scales=w_scales[s][:], in_=w_bf[s][:])

        def quantize_x(s, a, b):
            nc.vector.quantize_mx(
                out=x_codes[s][:, a:b].bitcast(FP8X4),
                scales=x_scales[s][:, a:b],
                in_=x_bf[s][:, PACK * a : PACK * b],
            )

        def products(s):
            for c in range(SIDE):
                rows = slice(ROWS * c, ROWS * (c + 1))
                nc.tensor.matmul_mx(
                    out=acc[SIDE * s + c][:],
                    lhsT=w_codes[s][rows, :].bitcast(FP8X4),
                    lhsT_scale=w_scales[s][rows, :],
                    rhs=x_codes[s][rows, :].bitcast(FP8X4),
                    rhs_scale=x_scales[s][rows, :],
                    start=True,
                    stop=True,
                )

        def silu(g):
            nc.scalar.activation(out=act[g][:], in_=acc[g][:], func=SILU)

        def finish(g):
            nc.vector.tensor_tensor(out=act[g][:], in0=act[g][:], in1=res_of[g], op=ADD)
            nc.sync.dma_start(out=out[g], in_=act[g][:])

        interleave_x(nc.scalar.copy, 0, SPLIT, N)
        interleave_x(nc.vector.tensor_copy, 0, 0, HALF)
        interleave_x(nc.vector.tensor_copy, 0, HALF, SPLIT)
        quantize_x(0, 0, HALF)
        quantize_x(0, HALF, N)
        interleave_w(nc.scalar.copy, 0)
        quantize_w(0)
        products(0)
        interleave_w(nc.vector.tensor_copy, 1)
        quantize_w(1)
        silu(0)
        interleave_x(nc.scalar.copy, 1, HALF, N)
        interleave_x(nc.vector.tensor_copy, 1, 0, HALF)
        finish(0)
        quantize_x(1, 0, HALF)
        quantize_x(1, HALF, N)
        products(1)
        for g in range(1, G):
            silu(g)
            finish(g)
